import numpy as np
import ml_dtypes


def mxq(x, axis, fmt="e4m3"):
    dtype, down = {"e4m3": (ml_dtypes.float8_e4m3fn, 7), "e5m2": (ml_dtypes.float8_e5m2, 14)}[fmt]
    v = np.moveaxis(np.asarray(x, np.float32).astype(ml_dtypes.bfloat16).astype(np.float64), axis, -1)
    blocks = v.reshape(v.shape[:-1] + (-1, 32))
    amax = np.abs(blocks).max(-1, keepdims=True)
    byte = np.maximum(np.where(amax > 0, np.frexp(amax)[1] - 1 + 127, 0) - down, 1)
    scale = np.exp2(byte - 127.0)
    codes = (blocks / scale).astype(np.float32).astype(dtype).astype(np.float64)
    return np.moveaxis((codes * scale).reshape(v.shape), -1, axis)


WIDE = False


def mx_kscale(k):
    if not WIDE:
        return np.ones(k)
    levels = np.array([10, -10, 5, -5, 0])
    if k % 512:
        return np.exp2(np.random.permutation(np.resize(levels, k // 32))).repeat(32)
    a = np.empty((k // 512, 16))
    for p in range(k // 512):
        a[p, :8] = np.random.permutation(np.resize(levels, 8))
        for g in range(8):
            far = levels[np.abs(levels - a[p, g]) >= 10]
            a[p, g + 8] = far[np.random.randint(len(far))]
    return np.exp2(a.ravel()).repeat(32)


def f64(x):
    return np.asarray(x).astype(np.float64)


def striped(idx):
    return np.tile(idx.reshape(-1, 16).T, (8, 1)).astype(np.uint16)


def unstriped(offs):
    return offs[:16].T.reshape(-1).astype(np.int64)


E2M1 = np.array([0.0, 0.5, 1.0, 1.5, 2.0, 3.0, 4.0, 6.0, -0.0, -0.5, -1.0, -1.5, -2.0, -3.0, -4.0, -6.0])


def pack_weight(w, fmt):
    k, n = w.shape
    w = f64(np.asarray(w, np.float32).astype(ml_dtypes.bfloat16)).reshape(k // 32, 32, n)
    amax = np.abs(w).max(1)
    if fmt == "e4m3":
        byte = np.frexp(amax)[1] - 1 + 127 - 7
    else:
        mant, ex = np.frexp(amax / 6.0)
        byte = np.where(mant > 0.5, ex, ex - 1) + 127
    byte = np.clip(np.where(amax > 0, byte, 1), 1, 254)
    scaled = (w * np.exp2(127.0 - byte)[:, None, :]).reshape(k, n).astype(np.float32)
    by_word = np.ascontiguousarray(scaled.reshape(k // 512, 128, 4, n).transpose(0, 1, 3, 2))
    if fmt == "e4m3":
        words = by_word.astype(ml_dtypes.float8_e4m3fn).view(np.uint8)
    else:
        c = by_word.astype(ml_dtypes.float4_e2m1fn).view(np.uint8) & 0xF
        words = (c[..., 0::2] | (c[..., 1::2] << 4)).reshape(k // 512, 128, 2 * n)
    return np.ascontiguousarray(words), np.ascontiguousarray(byte.astype(np.uint8).reshape(k // 512, 16, n))


def unpack_weight(words, scales, fmt):
    g, _, n = scales.shape
    words = np.ascontiguousarray(words).reshape(g, 128, n, -1)
    if fmt == "e4m3":
        vals = words.view(ml_dtypes.float8_e4m3fn).astype(np.float64)
    else:
        nib = np.empty((g, 128, n, 4), np.uint8)
        nib[..., 0::2] = words & 0xF
        nib[..., 1::2] = words >> 4
        vals = E2M1[nib]
    vals = vals * np.repeat(np.exp2(scales.astype(np.float64) - 127.0), 8, axis=1)[..., None]
    return vals.transpose(0, 1, 3, 2).reshape(g * 512, n)


def gelu(v):
    return 0.5 * v * (1.0 + np.tanh(np.sqrt(2.0 / np.pi) * (v + 0.044715 * v**3)))


K, H, N, T, S = 1024, 1024, 512, 2048, 512

def setup_inputs():
    n = np.random.standard_normal
    s = mx_kscale(K)[:, None]
    u = mx_kscale(H)[:, None]
    tab_words, tab_scales = pack_weight(n((K, T)) * s, "e4m3")
    w2_words, w2_scales = pack_weight(n((K, H)) / np.sqrt(K) / s * u.T, "e4m3")
    w4_words, w4_scales = pack_weight(n((H, N)) / np.sqrt(H) / u, "e2m1")
    return {
        "tab_words": tab_words, "tab_scales": tab_scales,
        "offs": striped(np.random.permutation(T)[:S]),
        "offs2": striped(np.random.permutation(T)[:S]),
        "offs3": striped(np.random.permutation(T)[:S]),
        "w1": (0.38 * n((K, H)) / np.sqrt(K) / s).astype(np.float32),
        "b1": np.random.uniform(-1.0, 1.0, H).astype(np.float32),
        "w2_words": w2_words, "w2_scales": w2_scales,
        "w3": (n((K, H)) / np.sqrt(K) / s * u.T).astype(np.float32),
        "b3": (0.5 * n(H) * u[:, 0]).astype(np.float32),
        "w4_words": w4_words, "w4_scales": w4_scales,
        "w5": (n((H, N)) / np.sqrt(H) / u).astype(np.float32),
        "b5": (0.5 * n(N)).astype(np.float32),
    }

def reference(tab_words, tab_scales, offs, offs2, offs3, w1, b1, w2_words, w2_scales, w3, b3, w4_words, w4_scales, w5, b5):
    TW = unpack_weight(tab_words, tab_scales, "e4m3")
    v = TW[:, unstriped(offs)]
    v2 = TW[:, unstriped(offs2)]
    v3 = TW[:, unstriped(offs3)]
    w2 = unpack_weight(w2_words, w2_scales, "e4m3")
    w4 = unpack_weight(w4_words, w4_scales, "e2m1")
    drug = (mxq(f64(w1), 0, "e4m3").T @ v) + f64(b1)[:, None]
    cof = w2.T @ v2
    sol = (mxq(f64(w3), 0, "e4m3").T @ v3) + f64(b3)[:, None]
    h1 = np.cos(drug) * cof
    h2 = np.maximum(cof, sol)
    h1q = mxq(h1, 0, "e4m3")
    h2q = mxq(h2, 0, "e4m3")
    y = w4.T @ h1q + mxq(f64(w5), 0, "e4m3").T @ h2q
    return np.tanh(y + f64(b5)[:, None])

@@ -1,0 +1,305 @@
+import math
+from contextlib import ExitStack
+
+import concourse.mybir as mybir
+
+K, H, N, T, S = 1024, 1024, 512, 2048, 512
+FLOPS = 2 * S * (3 * K * H + 2 * H * N)
+
+F32 = mybir.dt.float32
+BF16 = mybir.dt.bfloat16
+I32 = mybir.dt.int32
+U32 = mybir.dt.uint32
+U16 = mybir.dt.uint16
+U8 = mybir.dt.uint8
+FP8X4 = mybir.dt.float8_e4m3fn_x4
+FP4X4 = mybir.dt.float4_e2m1fn_x4
+ACT = mybir.ActivationFunctionType
+ALU = mybir.AluOpType
+
+P = 128
+PACK = 4
+PASS = P * PACK
+QUADS = 4
+JW = 128
+JQ = S // JW
+
+
+def tile_list_cocrystal_former_screen_kernel(
+    tc, tab_words, tab_scales, offs, offs2, offs3, w1, b1, w2_words, w2_scales, w3, b3, w4_words, w4_scales, w5, b5, out
+):
+    nc = tc.nc
+    with ExitStack() as ctx:
+        keep = ctx.enter_context(tc.tile_pool(name="keep", bufs=1))
+        raw_pool = ctx.enter_context(tc.tile_pool(name="raw", bufs=8))
+        round_pool = ctx.enter_context(tc.tile_pool(name="rounded", bufs=3))
+        work = ctx.enter_context(tc.tile_pool(name="work", bufs=3))
+        cof_psum = ctx.enter_context(tc.psum_pool(name="cof_psum", bufs=1))
+        acc_psum = ctx.enter_context(tc.psum_pool(name="acc_psum", bufs=2))
+        y_psum = ctx.enter_context(tc.psum_pool(name="y_psum", bufs=2))
+
+        def kept(shape, dtype, name):
+            return keep.tile(shape, dtype, name=name, align_bytes=64)
+
+        lists = [kept([P, S // 16], U16, "list%d" % i) for i in range(3)]
+        tab = [kept([P, T], U32, "tab%d" % a) for a in range(2)]
+        tab_sc = kept([P, T], U8, "tab_sc")
+        w2_raw = kept([P, 2, H], U32, "w2_raw")
+        w2_sc_raw = kept([P, H], U8, "w2_sc_raw")
+        w4 = kept([P, 2, 2 * N], U8, "w4")
+        w4_sc = kept([P, 2, N], U8, "w4_sc")
+        b1_sb = kept([P, 2, PACK], F32, "b1_sb")
+        b3_sb = kept([P, 2, PACK], F32, "b3_sb")
+        b5_sb = kept([P, N // P], F32, "b5_sb")
+
+        nc.gpsimd.memset(tab_sc[:].bitcast(I32), 0)
+        nc.vector.memset(w2_sc_raw[:].bitcast(I32), 0)
+        nc.vector.memset(w4_sc[:].rearrange("p a n -> p (a n)").bitcast(I32), 0)
+
+        raw = {}
+
+        def load_tab(a):
+            nc.sync.dma_start(out=tab[a][:].bitcast(I32), in_=tab_words[a].rearrange("p t i -> p (t i)").bitcast(I32))
+
+        def load_w(name, w, a, b):
+            raw[name, a, b] = raw_pool.tile([P, PACK, P, PACK], F32, name="raw")
+            rows = w[PASS * a : PASS * (a + 1), PASS * b : PASS * (b + 1)]
+            nc.sync.dma_start(out=raw[name, a, b][:], in_=rows.rearrange("(p j) (m t) -> p j m t", j=PACK, t=PACK))
+
+        nc.sync.dma_start(lists[0][:], offs)
+        nc.sync.dma_start(lists[2][:], offs3)
+        nc.sync.dma_start(lists[1][:], offs2)
+        nc.sync.dma_start(out=b1_sb[:], in_=b1.rearrange("(b p t) -> p b t", b=2, t=PACK))
+        load_tab(0)
+        load_w("w1", w1, 0, 0)
+        for q in range(QUADS):
+            nc.sync.dma_start(
+                out=tab_sc[32 * q : 32 * q + 8, :].bitcast(I32), in_=tab_scales[:, 4 * q : 4 * q + 4, :].bitcast(I32)
+            )
+        load_tab(1)
+        load_w("w1", w1, 1, 0)
+        load_w("w3", w3, 0, 0)
+        load_w("w3", w3, 1, 0)
+        for q in range(QUADS):
+            nc.sync.dma_start(
+                out=w2_sc_raw[32 * q : 32 * q + 8, :].bitcast(I32), in_=w2_scales[:, 4 * q : 4 * q + 4, :].bitcast(I32)
+            )
+        nc.sync.dma_start(out=w2_raw[:].bitcast(I32), in_=w2_words.rearrange("a p c i -> p a (c i)").bitcast(I32))
+        nc.sync.dma_start(out=b3_sb[:], in_=b3.rearrange("(b p t) -> p b t", b=2, t=PACK))
+        load_w("w1", w1, 0, 1)
+        load_w("w1", w1, 1, 1)
+        load_w("w3", w3, 0, 1)
+        load_w("w3", w3, 1, 1)
+        for q in range(QUADS):
+            nc.sync.dma_start(
+                out=w4_sc[32 * q : 32 * q + 4, :, :].bitcast(I32),
+                in_=w4_scales[:, 4 * q : 4 * q + 4, :].rearrange("a r n -> r a n").bitcast(I32),
+            )
+        nc.sync.dma_start(out=w4[:].bitcast(I32), in_=w4_words.rearrange("a p x -> p a x").bitcast(I32))
+        with nc.allow_non_contiguous_dma(reason="one bias value for each partition and output tile"):
+            nc.sync.dma_start(out=b5_sb[:], in_=b5.rearrange("(c p) -> p c", p=P))
+
+        picked = {}
+        picked_sc = {}
+
+        def gather_words(i, a, tag=""):
+            picked[i, a] = keep.tile([P, S], U32, name="picked%d_%d" % (i, a), tag=tag, align_bytes=64)
+            nc.vector.tensor_copy(picked[i, a][:], tab[a][:].indirect(lists[i][:]))
+
+        def gather_scales(i):
+            picked_sc[i] = kept([P, S], U8, "picked_sc%d" % i)
+            nc.vector.tensor_copy(picked_sc[i][:], tab_sc[:].indirect(lists[i][:]))
+
+        rounded = {}
+        codes = {}
+        scales = {}
+
+        def round_w(name, a, b, engines, tag=""):
+            pool = keep if tag else round_pool
+            rounded[name, a, b] = pool.tile([P, PASS * PACK], BF16, name="rounded", tag=tag, align_bytes=64)
+            for half, engine in enumerate(engines):
+                dst = rounded[name, a, b][:, 2 * PASS * half : 2 * PASS * (half + 1)]
+                if name == "w5":
+                    src = raw[name, a, b][:, :, 64 * half : 64 * (half + 1), :].rearrange("p j g i -> p g j i")
+                    dst = dst.rearrange("p (g i j) -> p g j i", i=4, j=PACK)
+                else:
+                    src = raw[name, a, b][:, :, :, 2 * half : 2 * (half + 1)].rearrange("p j m t -> p m j t")
+                    dst = dst.rearrange("p (t m j) -> p m j t", t=2, j=PACK)
+                if engine == "V":
+                    nc.vector.tensor_copy(out=dst, in_=src)
+                else:
+                    nc.scalar.copy(out=dst, in_=src)
+
+        def quantize_w(name, a, b):
+            codes[name, a, b] = kept([P, PASS], U32, "%s_codes%d%d" % (name, a, b))
+            scales[name, a, b] = kept([P, PASS], U8, "%s_scales%d%d" % (name, a, b))
+            nc.vector.quantize_mx(
+                out=codes[name, a, b][:].bitcast(FP8X4), scales=scales[name, a, b][:], in_=rounded[name, a, b][:]
+            )
+
+        def first_stage(name, i, b, t):
+            acc = acc_psum.tile([P, S], F32, name="acc")
+            cols = slice(P * t, P * (t + 1))
+            for a in range(2):
+                nc.tensor.matmul_mx(
+                    out=acc[:],
+                    lhsT=codes[name, a, b][:, cols].bitcast(FP8X4),
+                    lhsT_scale=scales[name, a, b][:, cols],
+                    rhs=picked[i, a][:].bitcast(FP8X4),
+                    rhs_scale=picked_sc[i][4 * a :, :],
+                    start=(a == 0),
+                    stop=(a == 1),
+                )
+            return acc
+
+        cos_drug = {}
+        sol = {}
+
+        def drug_stage(b):
+            cos_drug[b] = kept([P, PACK, S], F32, "cos_drug%d" % b)
+            for t in range(PACK):
+                acc = first_stage("w1", 0, b, t)
+                mag = work.tile([P, S], F32, name="mag")
+                nc.scalar.activation(out=mag[:], in_=acc[:], func=ACT.Abs, bias=b1_sb[:, b, t : t + 1])
+                nc.scalar.activation(out=cos_drug[b][:, t, :], in_=mag[:], func=ACT.Sin, scale=-1.0, bias=math.pi / 2)
+
+        def sol_stage(b):
+            sol[b] = kept([P, PACK, S], F32, "sol%d" % b)
+            for t in range(PACK):
+                acc = first_stage("w3", 2, b, t)
+                nc.scalar.activation(out=sol[b][:, t, :], in_=acc[:], func=ACT.Identity, bias=b3_sb[:, b, t : t + 1])
+
+        w2 = kept([P, 2, H], U32, "w2")
+        w2_sc = kept([P, H], U8, "w2_sc")
+
+        def deal_w2():
+            for a in range(2):
+                nc.vector.tensor_copy(
+                    out=w2[:, a, :].rearrange("p (t g i) -> p g t i", t=PACK, i=4),
+                    in_=w2_raw[:, a, :].rearrange("p (g i t) -> p g t i", t=PACK, i=4),
+                )
+            nc.vector.tensor_copy(
+                out=w2_sc[:].rearrange("p (t g i) -> p g t i", t=PACK, i=16),
+                in_=w2_sc_raw[:].rearrange("p (g i t) -> p g t i", t=PACK, i=16),
+            )
+
+        cof = {}
+
+        def cof_stage(b, jq):
+            cof[b, jq] = cof_psum.tile([P, PACK, JW], F32, name="cof%d" % jq)
+            js = slice(JW * jq, JW * (jq + 1))
+            for t in range(PACK):
+                cols = slice(2 * P * t + P * b, 2 * P * t + P * (b + 1))
+                for a in range(2):
+                    nc.tensor.matmul_mx(
+                        out=cof[b, jq][:, t, :],
+                        lhsT=w2[:, a, cols].bitcast(FP8X4),
+                        lhsT_scale=w2_sc[4 * a :, cols],
+                        rhs=picked[1, a][:, js].bitcast(FP8X4),
+                        rhs_scale=picked_sc[1][4 * a :, js],
+                        start=(a == 0),
+                        stop=(a == 1),
+                    )
+
+        h_rounded = {}
+
+        def combine(name, b, jq):
+            if jq == 0:
+                h_rounded[name, b] = work.tile([P, S * PACK], BF16, name="h_rounded", align_bytes=64)
+            other, op = (cos_drug[b], ALU.mult) if name == "h1" else (sol[b], ALU.max)
+            nc.vector.tensor_tensor(
+                out=h_rounded[name, b][:, PACK * JW * jq : PACK * JW * (jq + 1)].rearrange(
+                    "p (g i t) -> p g t i", t=PACK, i=4
+                ),
+                in0=other[:, :, JW * jq : JW * (jq + 1)].rearrange("p t (g i) -> p g t i", i=4),
+                in1=cof[b, jq][:].rearrange("p t (g i) -> p g t i", i=4),
+                op=op,
+            )
+
+        def quantize_h(name, b, j0, j1):
+            if j0 == 0:
+                codes[name, b] = kept([P, S], U32, "%s_codes%d" % (name, b))
+                scales[name, b] = kept([P, S], U8, "%s_scales%d" % (name, b))
+            nc.vector.quantize_mx(
+                out=codes[name, b][:, j0:j1].bitcast(FP8X4),
+                scales=scales[name, b][:, j0:j1],
+                in_=h_rounded[name, b][:, PACK * j0 : PACK * j1],
+            )
+
+        def second_stage(jq):
+            if jq < 2:
+                y = y_psum.tile([P, N // P, JW], F32, name="y")
+            else:
+                y = acc_psum.tile([P, N // P, JW], F32, name="y", tag="acc")
+            js = slice(JW * jq, JW * (jq + 1))
+            passes = [(b, name, c) for b in range(2) for name in ("h1", "h2") for c in range(N // P)]
+            for n, (b, name, c) in enumerate(passes):
+                cols = slice(P * c, P * (c + 1))
+                if name == "h1":
+                    lhsT = w4[:, b, 2 * P * c : 2 * P * (c + 1)].bitcast(FP4X4)
+                    lhsT_scale = w4_sc[:, b, cols]
+                else:
+                    lhsT = codes["w5", b, 0][:, cols].bitcast(FP8X4)
+                    lhsT_scale = scales["w5", b, 0][:, cols]
+                nc.tensor.matmul_mx(
+                    out=y[:, c, :],
+                    lhsT=lhsT,
+                    lhsT_scale=lhsT_scale,
+                    rhs=codes[name, b][:, js].bitcast(FP8X4),
+                    rhs_scale=scales[name, b][:, js],
+                    start=(n == 0),
+                    stop=(n == len(passes) - 1),
+                )
+            scores = work.tile([P, N // P, JW], F32, name="scores", bufs=JQ)
+            for c in range(N // P):
+                nc.scalar.activation(out=scores[:, c, :], in_=y[:, c, :], func=ACT.Tanh, bias=b5_sb[:, c : c + 1])
+            nc.sync.dma_start(out=out[:, js].rearrange("(c p) j -> p c j", p=P), in_=scores[:])
+
+        gather_words(0, 0)
+        gather_scales(0)
+        for a in range(2):
+            round_w("w1", a, 0, "SS", "first%d" % a)
+            quantize_w("w1", a, 0)
+        gather_words(0, 1)
+        drug_stage(0)
+        gather_words(2, 0)
+        gather_scales(2)
+        gather_words(2, 1, "first1")
+        for a in range(2):
+            round_w("w3", a, 0, ("SS", "SV")[a])
+            quantize_w("w3", a, 0)
+        sol_stage(0)
+        gather_words(1, 0)
+        gather_scales(1)
+        gather_words(1, 1, "first0")
+        deal_w2()
+        load_w("w5", w5, 0, 0)
+        load_w("w5", w5, 1, 0)
+        for a in range(2):
+            round_w("w1", a, 1, ("SV", "SV")[a])
+            quantize_w("w1", a, 1)
+        drug_stage(1)
+        for a in range(2):
+            round_w("w3", a, 1, ("SV", "SV")[a])
+            quantize_w("w3", a, 1)
+        sol_stage(1)
+        for jq in range(JQ):
+            cof_stage(0, jq)
+            combine("h1", 0, jq)
+            combine("h2", 0, jq)
+        quantize_h("h1", 0, 0, S)
+        quantize_h("h2", 0, 0, S)
+        for jq in range(JQ):
+            cof_stage(1, jq)
+            combine("h1", 1, jq)
+        for b in range(2):
+            round_w("w5", b, 0, ("SV", "SV")[b])
+            quantize_w("w5", b, 0)
+        quantize_h("h1", 1, 0, S)
+        for jq in range(JQ):
+            combine("h2", 1, jq)
+            if jq > 0:
+                quantize_h("h2", 1, JW * (jq - 1), JW * jq)
+                second_stage(jq - 1)
+        quantize_h("h2", 1, JW * (JQ - 1), S)
+        second_stage(JQ - 1)

@@ -31,12 +31,10 @@ def tile_list_cocrystal_former_screen_kernel(
     nc = tc.nc
     with ExitStack() as ctx:
         keep = ctx.enter_context(tc.tile_pool(name="keep", bufs=1))
-        raw_pool = ctx.enter_context(tc.tile_pool(name="raw", bufs=8))
+        raw_pool = ctx.enter_context(tc.tile_pool(name="raw", bufs=6))
         round_pool = ctx.enter_context(tc.tile_pool(name="rounded", bufs=3))
         work = ctx.enter_context(tc.tile_pool(name="work", bufs=3))
-        cof_psum = ctx.enter_context(tc.psum_pool(name="cof_psum", bufs=1))
-        acc_psum = ctx.enter_context(tc.psum_pool(name="acc_psum", bufs=2))
-        y_psum = ctx.enter_context(tc.psum_pool(name="y_psum", bufs=2))
+        psum = ctx.enter_context(tc.psum_pool(name="psum", bufs=1))
 
         def kept(shape, dtype, name):
             return keep.tile(shape, dtype, name=name, align_bytes=64)
@@ -44,7 +42,6 @@ def tile_list_cocrystal_former_screen_kernel(
         lists = [kept([P, S // 16], U16, "list%d" % i) for i in range(3)]
         tab = [kept([P, T], U32, "tab%d" % a) for a in range(2)]
         tab_sc = kept([P, T], U8, "tab_sc")
-        w2_raw = kept([P, 2, H], U32, "w2_raw")
         w2_sc_raw = kept([P, H], U8, "w2_sc_raw")
         w4 = kept([P, 2, 2 * N], U8, "w4")
         w4_sc = kept([P, 2, N], U8, "w4_sc")
@@ -56,54 +53,28 @@ def tile_list_cocrystal_former_screen_kernel(
         nc.vector.memset(w2_sc_raw[:].bitcast(I32), 0)
         nc.vector.memset(w4_sc[:].rearrange("p a n -> p (a n)").bitcast(I32), 0)
 
+        warm = kept([P, 1], F32, "warm")
+        nc.vector.memset(warm[:], 0.0)
+        nc.scalar.activation(out=warm[:], in_=warm[:], func=ACT.Silu)
+
         raw = {}
 
         def load_tab(a):
             nc.sync.dma_start(out=tab[a][:].bitcast(I32), in_=tab_words[a].rearrange("p t i -> p (t i)").bitcast(I32))
 
         def load_w(name, w, a, b):
-            raw[name, a, b] = raw_pool.tile([P, PACK, P, PACK], F32, name="raw")
+            if (name, a, b) in (("w3", 0, 0), ("w3", 0, 1),):
+                raw[name, a, b] = keep.tile([P, PACK, P, PACK], F32, name="raw", tag="scratch%d" % b)
+            else:
+                raw[name, a, b] = raw_pool.tile([P, PACK, P, PACK], F32, name="raw")
             rows = w[PASS * a : PASS * (a + 1), PASS * b : PASS * (b + 1)]
             nc.sync.dma_start(out=raw[name, a, b][:], in_=rows.rearrange("(p j) (m t) -> p j m t", j=PACK, t=PACK))
-
-        nc.sync.dma_start(lists[0][:], offs)
-        nc.sync.dma_start(lists[2][:], offs3)
-        nc.sync.dma_start(lists[1][:], offs2)
-        nc.sync.dma_start(out=b1_sb[:], in_=b1.rearrange("(b p t) -> p b t", b=2, t=PACK))
-        load_tab(0)
-        load_w("w1", w1, 0, 0)
-        for q in range(QUADS):
-            nc.sync.dma_start(
-                out=tab_sc[32 * q : 32 * q + 8, :].bitcast(I32), in_=tab_scales[:, 4 * q : 4 * q + 4, :].bitcast(I32)
-            )
-        load_tab(1)
-        load_w("w1", w1, 1, 0)
-        load_w("w3", w3, 0, 0)
-        load_w("w3", w3, 1, 0)
-        for q in range(QUADS):
-            nc.sync.dma_start(
-                out=w2_sc_raw[32 * q : 32 * q + 8, :].bitcast(I32), in_=w2_scales[:, 4 * q : 4 * q + 4, :].bitcast(I32)
-            )
-        nc.sync.dma_start(out=w2_raw[:].bitcast(I32), in_=w2_words.rearrange("a p c i -> p a (c i)").bitcast(I32))
-        nc.sync.dma_start(out=b3_sb[:], in_=b3.rearrange("(b p t) -> p b t", b=2, t=PACK))
-        load_w("w1", w1, 0, 1)
-        load_w("w1", w1, 1, 1)
-        load_w("w3", w3, 0, 1)
-        load_w("w3", w3, 1, 1)
-        for q in range(QUADS):
-            nc.sync.dma_start(
-                out=w4_sc[32 * q : 32 * q + 4, :, :].bitcast(I32),
-                in_=w4_scales[:, 4 * q : 4 * q + 4, :].rearrange("a r n -> r a n").bitcast(I32),
-            )
-        nc.sync.dma_start(out=w4[:].bitcast(I32), in_=w4_words.rearrange("a p x -> p a x").bitcast(I32))
-        with nc.allow_non_contiguous_dma(reason="one bias value for each partition and output tile"):
-            nc.sync.dma_start(out=b5_sb[:], in_=b5.rearrange("(c p) -> p c", p=P))
 
         picked = {}
         picked_sc = {}
 
-        def gather_words(i, a, tag=""):
-            picked[i, a] = keep.tile([P, S], U32, name="picked%d_%d" % (i, a), tag=tag, align_bytes=64)
+        def gather_words(i, a):
+            picked[i, a] = kept([P, S], U32, "picked%d_%d" % (i, a))
             nc.vector.tensor_copy(picked[i, a][:], tab[a][:].indirect(lists[i][:]))
 
         def gather_scales(i):
@@ -114,9 +85,8 @@ def tile_list_cocrystal_former_screen_kernel(
         codes = {}
         scales = {}
 
-        def round_w(name, a, b, engines, tag=""):
-            pool = keep if tag else round_pool
-            rounded[name, a, b] = pool.tile([P, PASS * PACK], BF16, name="rounded", tag=tag, align_bytes=64)
+        def round_w(name, a, b, engines):
+            rounded[name, a, b] = round_pool.tile([P, PASS * PACK], BF16, name="rounded", align_bytes=64)
             for half, engine in enumerate(engines):
                 dst = rounded[name, a, b][:, 2 * PASS * half : 2 * PASS * (half + 1)]
                 if name == "w5":
@@ -137,8 +107,8 @@ def tile_list_cocrystal_former_screen_kernel(
                 out=codes[name, a, b][:].bitcast(FP8X4), scales=scales[name, a, b][:], in_=rounded[name, a, b][:]
             )
 
-        def first_stage(name, i, b, t):
-            acc = acc_psum.tile([P, S], F32, name="acc")
+        def first_stage(name, i, b, t, bank):
+            acc = psum.tile([P, S], F32, name="acc", tag="bank%d" % bank)
             cols = slice(P * t, P * (t + 1))
             for a in range(2):
                 nc.tensor.matmul_mx(
@@ -157,18 +127,20 @@ def tile_list_cocrystal_former_screen_kernel(
 
         def drug_stage(b):
             cos_drug[b] = kept([P, PACK, S], F32, "cos_drug%d" % b)
+            mags = keep.tile([P, 2, S], F32, name="mags", tag="scratch%d" % b)
             for t in range(PACK):
-                acc = first_stage("w1", 0, b, t)
-                mag = work.tile([P, S], F32, name="mag")
-                nc.scalar.activation(out=mag[:], in_=acc[:], func=ACT.Abs, bias=b1_sb[:, b, t : t + 1])
-                nc.scalar.activation(out=cos_drug[b][:, t, :], in_=mag[:], func=ACT.Sin, scale=-1.0, bias=math.pi / 2)
+                acc = first_stage("w1", 0, b, t, 4 * b + t)
+                mag = mags[:, t % 2, :]
+                nc.scalar.activation(out=mag, in_=acc[:], func=ACT.Abs, bias=b1_sb[:, b, t : t + 1])
+                nc.scalar.activation(out=cos_drug[b][:, t, :], in_=mag, func=ACT.Sin, scale=-1.0, bias=math.pi / 2)
 
         def sol_stage(b):
             sol[b] = kept([P, PACK, S], F32, "sol%d" % b)
             for t in range(PACK):
-                acc = first_stage("w3", 2, b, t)
+                acc = first_stage("w3", 2, b, t, 4 + t if b == 0 else 6 + t % 2)
                 nc.scalar.activation(out=sol[b][:, t, :], in_=acc[:], func=ACT.Identity, bias=b3_sb[:, b, t : t + 1])
 
+        w2_raw = kept([P, 2, H], U32, "w2_raw")
         w2 = kept([P, 2, H], U32, "w2")
         w2_sc = kept([P, H], U8, "w2_sc")
 
@@ -186,7 +158,7 @@ def tile_list_cocrystal_former_screen_kernel(
         cof = {}
 
         def cof_stage(b, jq):
-            cof[b, jq] = cof_psum.tile([P, PACK, JW], F32, name="cof%d" % jq)
+            cof[b, jq] = psum.tile([P, PACK, JW], F32, name="cof", tag="bank%d" % jq)
             js = slice(JW * jq, JW * (jq + 1))
             for t in range(PACK):
                 cols = slice(2 * P * t + P * b, 2 * P * t + P * (b + 1))
@@ -227,10 +199,7 @@ def tile_list_cocrystal_former_screen_kernel(
             )
 
         def second_stage(jq):
-            if jq < 2:
-                y = y_psum.tile([P, N // P, JW], F32, name="y")
-            else:
-                y = acc_psum.tile([P, N // P, JW], F32, name="y", tag="acc")
+            y = psum.tile([P, N // P, JW], F32, name="y", tag="bank%d" % (4 + jq))
             js = slice(JW * jq, JW * (jq + 1))
             passes = [(b, name, c) for b in range(2) for name in ("h1", "h2") for c in range(N // P)]
             for n, (b, name, c) in enumerate(passes):
@@ -255,46 +224,86 @@ def tile_list_cocrystal_former_screen_kernel(
                 nc.scalar.activation(out=scores[:, c, :], in_=y[:, c, :], func=ACT.Tanh, bias=b5_sb[:, c : c + 1])
             nc.sync.dma_start(out=out[:, js].rearrange("(c p) j -> p c j", p=P), in_=scores[:])
 
-        gather_words(0, 0)
-        gather_scales(0)
-        for a in range(2):
-            round_w("w1", a, 0, "SS", "first%d" % a)
-            quantize_w("w1", a, 0)
-        gather_words(0, 1)
-        drug_stage(0)
-        gather_words(2, 0)
-        gather_scales(2)
-        gather_words(2, 1, "first1")
-        for a in range(2):
-            round_w("w3", a, 0, ("SS", "SV")[a])
-            quantize_w("w3", a, 0)
-        sol_stage(0)
-        gather_words(1, 0)
-        gather_scales(1)
-        gather_words(1, 1, "first0")
-        deal_w2()
+        nc.sync.dma_start(lists[0][:], offs)
+        nc.sync.dma_start(lists[2][:], offs3)
+        nc.sync.dma_start(lists[1][:], offs2)
+        nc.sync.dma_start(out=b1_sb[:], in_=b1.rearrange("(b p t) -> p b t", b=2, t=PACK))
+        load_tab(0)
+        load_w("w1", w1, 0, 0)
+        for q in range(QUADS):
+            nc.sync.dma_start(
+                out=tab_sc[32 * q : 32 * q + 8, :].bitcast(I32), in_=tab_scales[:, 4 * q : 4 * q + 4, :].bitcast(I32)
+            )
+        load_w("w1", w1, 1, 0)
+        load_tab(1)
+        load_w("w3", w3, 0, 0)
+        nc.sync.dma_start(out=b3_sb[:], in_=b3.rearrange("(b p t) -> p b t", b=2, t=PACK))
+        load_w("w3", w3, 1, 0)
+        for q in range(QUADS):
+            nc.sync.dma_start(
+                out=w2_sc_raw[32 * q : 32 * q + 8, :].bitcast(I32), in_=w2_scales[:, 4 * q : 4 * q + 4, :].bitcast(I32)
+            )
+        nc.sync.dma_start(out=w2_raw[:].bitcast(I32), in_=w2_words.rearrange("a p c i -> p a (c i)").bitcast(I32))
+        load_w("w1", w1, 0, 1)
+        load_w("w1", w1, 1, 1)
+        load_w("w3", w3, 0, 1)
+        load_w("w3", w3, 1, 1)
+        for q in range(QUADS):
+            nc.sync.dma_start(
+                out=w4_sc[32 * q : 32 * q + 4, :, :].bitcast(I32),
+                in_=w4_scales[:, 4 * q : 4 * q + 4, :].rearrange("a r n -> r a n").bitcast(I32),
+            )
+        nc.sync.dma_start(out=w4[:].bitcast(I32), in_=w4_words.rearrange("a p x -> p a x").bitcast(I32))
+        with nc.allow_non_contiguous_dma(reason="one bias value for each partition and output tile"):
+            nc.sync.dma_start(out=b5_sb[:], in_=b5.rearrange("(c p) -> p c", p=P))
         load_w("w5", w5, 0, 0)
         load_w("w5", w5, 1, 0)
-        for a in range(2):
-            round_w("w1", a, 1, ("SV", "SV")[a])
-            quantize_w("w1", a, 1)
-        drug_stage(1)
-        for a in range(2):
-            round_w("w3", a, 1, ("SV", "SV")[a])
-            quantize_w("w3", a, 1)
-        sol_stage(1)
+        gather_words(0, 0)
+        gather_words(2, 0)
+        gather_words(1, 0)
+        gather_scales(0)
+        gather_scales(2)
+        gather_scales(1)
+        round_w("w1", 0, 0, "SS")
+        quantize_w("w1", 0, 0)
+        round_w("w1", 1, 0, "SS")
+        quantize_w("w1", 1, 0)
+        gather_words(0, 1)
+        gather_words(2, 1)
+        gather_words(1, 1)
+        round_w("w3", 0, 0, "SS")
+        drug_stage(0)
+        quantize_w("w3", 0, 0)
+        round_w("w3", 1, 0, "VV")
+        quantize_w("w3", 1, 0)
+        sol_stage(0)
+        deal_w2()
         for jq in range(JQ):
             cof_stage(0, jq)
+        round_w("w1", 0, 1, "SS")
+        quantize_w("w1", 0, 1)
+        round_w("w1", 1, 1, "SV")
+        quantize_w("w1", 1, 1)
+        round_w("w3", 0, 1, "SS")
+        drug_stage(1)
+        quantize_w("w3", 0, 1)
+        round_w("w3", 1, 1, "VV")
+        quantize_w("w3", 1, 1)
+        sol_stage(1)
+        for jq in range(JQ):
             combine("h1", 0, jq)
+        for jq in range(JQ):
             combine("h2", 0, jq)
         quantize_h("h1", 0, 0, S)
         quantize_h("h2", 0, 0, S)
         for jq in range(JQ):
             cof_stage(1, jq)
+        round_w("w5", 0, 0, "VV")
+        quantize_w("w5", 0, 0)
+        round_w("w5", 1, 0, "SS")
+        quantize_w("w5", 1, 0)
+        for jq in range(JQ):
             combine("h1", 1, jq)
-        for b in range(2):
-            round_w("w5", b, 0, ("SV", "SV")[b])
-            quantize_w("w5", b, 0)
         quantize_h("h1", 1, 0, S)
         for jq in range(JQ):
             combine("h2", 1, jq)

@@ -90,8 +90,8 @@ def tile_list_cocrystal_former_screen_kernel(
             for half, engine in enumerate(engines):
                 dst = rounded[name, a, b][:, 2 * PASS * half : 2 * PASS * (half + 1)]
                 if name == "w5":
-                    src = raw[name, a, b][:, :, 64 * half : 64 * (half + 1), :].rearrange("p j g i -> p g j i")
-                    dst = dst.rearrange("p (g i j) -> p g j i", i=4, j=PACK)
+                    src = raw[name, a, b][:, :, 64 * half : 64 * (half + 1), :].rearrange("p j g (u i) -> p (g u) j i", i=2)
+                    dst = dst.rearrange("p (g i j) -> p g j i", i=2, j=PACK)
                 else:
                     src = raw[name, a, b][:, :, :, 2 * half : 2 * (half + 1)].rearrange("p j m t -> p m j t")
                     dst = dst.rearrange("p (t m j) -> p m j t", t=2, j=PACK)
@@ -181,10 +181,10 @@ def tile_list_cocrystal_former_screen_kernel(
             other, op = (cos_drug[b], ALU.mult) if name == "h1" else (sol[b], ALU.max)
             nc.vector.tensor_tensor(
                 out=h_rounded[name, b][:, PACK * JW * jq : PACK * JW * (jq + 1)].rearrange(
-                    "p (g i t) -> p g t i", t=PACK, i=4
+                    "p (g i t) -> p g t i", t=PACK, i=2
                 ),
-                in0=other[:, :, JW * jq : JW * (jq + 1)].rearrange("p t (g i) -> p g t i", i=4),
-                in1=cof[b, jq][:].rearrange("p t (g i) -> p g t i", i=4),
+                in0=other[:, :, JW * jq : JW * (jq + 1)].rearrange("p t (g i) -> p g t i", i=2),
+                in1=cof[b, jq][:].rearrange("p t (g i) -> p g t i", i=2),
                 op=op,
             )
 
@@ -198,10 +198,15 @@ def tile_list_cocrystal_former_screen_kernel(
                 in_=h_rounded[name, b][:, PACK * j0 : PACK * j1],
             )
 
-        def second_stage(jq):
-            y = psum.tile([P, N // P, JW], F32, name="y", tag="bank%d" % (4 + jq))
+        ys = {}
+
+        def y_passes(jq, operands):
             js = slice(JW * jq, JW * (jq + 1))
-            passes = [(b, name, c) for b in range(2) for name in ("h1", "h2") for c in range(N // P)]
+            opens = jq not in ys
+            if opens:
+                ys[jq] = psum.tile([P, N // P, JW], F32, name="y", tag="bank%d" % (4 + jq))
+            y = ys[jq]
+            passes = [(b, name, c) for b, name in operands for c in range(N // P)]
             for n, (b, name, c) in enumerate(passes):
                 cols = slice(P * c, P * (c + 1))
                 if name == "h1":
@@ -216,9 +221,14 @@ def tile_list_cocrystal_former_screen_kernel(
                     lhsT_scale=lhsT_scale,
                     rhs=codes[name, b][:, js].bitcast(FP8X4),
                     rhs_scale=scales[name, b][:, js],
-                    start=(n == 0),
-                    stop=(n == len(passes) - 1),
+                    start=(opens and n == 0),
+                    stop=(not opens and n == len(passes) - 1),
                 )
+
+        def second_stage(jq):
+            js = slice(JW * jq, JW * (jq + 1))
+            y_passes(jq, [(1, "h2")])
+            y = ys[jq]
             scores = work.tile([P, N // P, JW], F32, name="scores", bufs=JQ)
             for c in range(N // P):
                 nc.scalar.activation(out=scores[:, c, :], in_=y[:, c, :], func=ACT.Tanh, bias=b5_sb[:, c : c + 1])
@@ -248,6 +258,8 @@ def tile_list_cocrystal_former_screen_kernel(
         load_w("w1", w1, 1, 1)
         load_w("w3", w3, 0, 1)
         load_w("w3", w3, 1, 1)
+        load_w("w5", w5, 0, 0)
+        load_w("w5", w5, 1, 0)
         for q in range(QUADS):
             nc.sync.dma_start(
                 out=w4_sc[32 * q : 32 * q + 4, :, :].bitcast(I32),
@@ -256,8 +268,6 @@ def tile_list_cocrystal_former_screen_kernel(
         nc.sync.dma_start(out=w4[:].bitcast(I32), in_=w4_words.rearrange("a p x -> p a x").bitcast(I32))
         with nc.allow_non_contiguous_dma(reason="one bias value for each partition and output tile"):
             nc.sync.dma_start(out=b5_sb[:], in_=b5.rearrange("(c p) -> p c", p=P))
-        load_w("w5", w5, 0, 0)
-        load_w("w5", w5, 1, 0)
         gather_words(0, 0)
         gather_words(2, 0)
         gather_words(1, 0)
@@ -305,6 +315,8 @@ def tile_list_cocrystal_former_screen_kernel(
         for jq in range(JQ):
             combine("h1", 1, jq)
         quantize_h("h1", 1, 0, S)
+        for jq in range(JQ):
+            y_passes(jq, [(0, "h1"), (0, "h2"), (1, "h1")])
         for jq in range(JQ):
             combine("h2", 1, jq)
             if jq > 0:

import math
from contextlib import ExitStack

import concourse.mybir as mybir

K, H, N, T, S = 1024, 1024, 512, 2048, 512
FLOPS = 2 * S * (3 * K * H + 2 * H * N)

F32 = mybir.dt.float32
BF16 = mybir.dt.bfloat16
I32 = mybir.dt.int32
U32 = mybir.dt.uint32
U16 = mybir.dt.uint16
U8 = mybir.dt.uint8
FP8X4 = mybir.dt.float8_e4m3fn_x4
FP4X4 = mybir.dt.float4_e2m1fn_x4
ACT = mybir.ActivationFunctionType
ALU = mybir.AluOpType

P = 128
PACK = 4
PASS = P * PACK
QUADS = 4
JW = 128
JQ = S // JW


def tile_list_cocrystal_former_screen_kernel(
    tc, tab_words, tab_scales, offs, offs2, offs3, w1, b1, w2_words, w2_scales, w3, b3, w4_words, w4_scales, w5, b5, out
):
    nc = tc.nc
    with ExitStack() as ctx:
        keep = ctx.enter_context(tc.tile_pool(name="keep", bufs=1))
        raw_pool = ctx.enter_context(tc.tile_pool(name="raw", bufs=6))
        round_pool = ctx.enter_context(tc.tile_pool(name="rounded", bufs=3))
        work = ctx.enter_context(tc.tile_pool(name="work", bufs=3))
        psum = ctx.enter_context(tc.psum_pool(name="psum", bufs=1))

        def kept(shape, dtype, name):
            return keep.tile(shape, dtype, name=name, align_bytes=64)

        lists = [kept([P, S // 16], U16, "list%d" % i) for i in range(3)]
        tab = [kept([P, T], U32, "tab%d" % a) for a in range(2)]
        tab_sc = kept([P, T], U8, "tab_sc")
        w2_sc_raw = kept([P, H], U8, "w2_sc_raw")
        w4 = kept([P, 2, 2 * N], U8, "w4")
        w4_sc = kept([P, 2, N], U8, "w4_sc")
        b1_sb = kept([P, 2, PACK], F32, "b1_sb")
        b3_sb = kept([P, 2, PACK], F32, "b3_sb")
        b5_sb = kept([P, N // P], F32, "b5_sb")

        nc.gpsimd.memset(tab_sc[:].bitcast(I32), 0)
        nc.vector.memset(w2_sc_raw[:].bitcast(I32), 0)
        nc.vector.memset(w4_sc[:].rearrange("p a n -> p (a n)").bitcast(I32), 0)

        warm = kept([P, 1], F32, "warm")
        nc.vector.memset(warm[:], 0.0)
        nc.scalar.activation(out=warm[:], in_=warm[:], func=ACT.Silu)

        raw = {}

        def load_tab(a):
            nc.sync.dma_start(out=tab[a][:].bitcast(I32), in_=tab_words[a].rearrange("p t i -> p (t i)").bitcast(I32))

        def load_w(name, w, a, b):
            if (name, a, b) in (("w3", 0, 0), ("w3", 0, 1),):
                raw[name, a, b] = keep.tile([P, PACK, P, PACK], F32, name="raw", tag="scratch%d" % b)
            else:
                raw[name, a, b] = raw_pool.tile([P, PACK, P, PACK], F32, name="raw")
            rows = w[PASS * a : PASS * (a + 1), PASS * b : PASS * (b + 1)]
            nc.sync.dma_start(out=raw[name, a, b][:], in_=rows.rearrange("(p j) (m t) -> p j m t", j=PACK, t=PACK))

        picked = {}
        picked_sc = {}

        def gather_words(i, a):
            picked[i, a] = kept([P, S], U32, "picked%d_%d" % (i, a))
            nc.vector.tensor_copy(picked[i, a][:], tab[a][:].indirect(lists[i][:]))

        def gather_scales(i):
            picked_sc[i] = kept([P, S], U8, "picked_sc%d" % i)
            nc.vector.tensor_copy(picked_sc[i][:], tab_sc[:].indirect(lists[i][:]))

        rounded = {}
        codes = {}
        scales = {}

        def round_w(name, a, b, engines):
            rounded[name, a, b] = round_pool.tile([P, PASS * PACK], BF16, name="rounded", align_bytes=64)
            for half, engine in enumerate(engines):
                dst = rounded[name, a, b][:, 2 * PASS * half : 2 * PASS * (half + 1)]
                if name == "w5":
                    src = raw[name, a, b][:, :, 64 * half : 64 * (half + 1), :].rearrange("p j g (u i) -> p (g u) j i", i=2)
                    dst = dst.rearrange("p (g i j) -> p g j i", i=2, j=PACK)
                else:
                    src = raw[name, a, b][:, :, :, 2 * half : 2 * (half + 1)].rearrange("p j m t -> p m j t")
                    dst = dst.rearrange("p (t m j) -> p m j t", t=2, j=PACK)
                if engine == "V":
                    nc.vector.tensor_copy(out=dst, in_=src)
                else:
                    nc.scalar.copy(out=dst, in_=src)

        def quantize_w(name, a, b):
            codes[name, a, b] = kept([P, PASS], U32, "%s_codes%d%d" % (name, a, b))
            scales[name, a, b] = kept([P, PASS], U8, "%s_scales%d%d" % (name, a, b))
            nc.vector.quantize_mx(
                out=codes[name, a, b][:].bitcast(FP8X4), scales=scales[name, a, b][:], in_=rounded[name, a, b][:]
            )

        def first_stage(name, i, b, t, bank):
            acc = psum.tile([P, S], F32, name="acc", tag="bank%d" % bank)
            cols = slice(P * t, P * (t + 1))
            for a in range(2):
                nc.tensor.matmul_mx(
                    out=acc[:],
                    lhsT=codes[name, a, b][:, cols].bitcast(FP8X4),
                    lhsT_scale=scales[name, a, b][:, cols],
                    rhs=picked[i, a][:].bitcast(FP8X4),
                    rhs_scale=picked_sc[i][4 * a :, :],
                    start=(a == 0),
                    stop=(a == 1),
                )
            return acc

        cos_drug = {}
        sol = {}

        def drug_stage(b):
            cos_drug[b] = kept([P, PACK, S], F32, "cos_drug%d" % b)
            mags = keep.tile([P, 2, S], F32, name="mags", tag="scratch%d" % b)
            for t in range(PACK):
                acc = first_stage("w1", 0, b, t, 4 * b + t)
                mag = mags[:, t % 2, :]
                nc.scalar.activation(out=mag, in_=acc[:], func=ACT.Abs, bias=b1_sb[:, b, t : t + 1])
                nc.scalar.activation(out=cos_drug[b][:, t, :], in_=mag, func=ACT.Sin, scale=-1.0, bias=math.pi / 2)

        def sol_stage(b):
            sol[b] = kept([P, PACK, S], F32, "sol%d" % b)
            for t in range(PACK):
                acc = first_stage("w3", 2, b, t, 4 + t if b == 0 else 6 + t % 2)
                nc.scalar.activation(out=sol[b][:, t, :], in_=acc[:], func=ACT.Identity, bias=b3_sb[:, b, t : t + 1])

        w2_raw = kept([P, 2, H], U32, "w2_raw")
        w2 = kept([P, 2, H], U32, "w2")
        w2_sc = kept([P, H], U8, "w2_sc")

        def deal_w2():
            for a in range(2):
                nc.vector.tensor_copy(
                    out=w2[:, a, :].rearrange("p (t g i) -> p g t i", t=PACK, i=4),
                    in_=w2_raw[:, a, :].rearrange("p (g i t) -> p g t i", t=PACK, i=4),
                )
            nc.vector.tensor_copy(
                out=w2_sc[:].rearrange("p (t g i) -> p g t i", t=PACK, i=16),
                in_=w2_sc_raw[:].rearrange("p (g i t) -> p g t i", t=PACK, i=16),
            )

        cof = {}

        def cof_stage(b, jq):
            cof[b, jq] = psum.tile([P, PACK, JW], F32, name="cof", tag="bank%d" % jq)
            js = slice(JW * jq, JW * (jq + 1))
            for t in range(PACK):
                cols = slice(2 * P * t + P * b, 2 * P * t + P * (b + 1))
                for a in range(2):
                    nc.tensor.matmul_mx(
                        out=cof[b, jq][:, t, :],
                        lhsT=w2[:, a, cols].bitcast(FP8X4),
                        lhsT_scale=w2_sc[4 * a :, cols],
                        rhs=picked[1, a][:, js].bitcast(FP8X4),
                        rhs_scale=picked_sc[1][4 * a :, js],
                        start=(a == 0),
                        stop=(a == 1),
                    )

        h_rounded = {}

        def combine(name, b, jq):
            if jq == 0:
                h_rounded[name, b] = work.tile([P, S * PACK], BF16, name="h_rounded", align_bytes=64)
            other, op = (cos_drug[b], ALU.mult) if name == "h1" else (sol[b], ALU.max)
            nc.vector.tensor_tensor(
                out=h_rounded[name, b][:, PACK * JW * jq : PACK * JW * (jq + 1)].rearrange(
                    "p (g i t) -> p g t i", t=PACK, i=2
                ),
                in0=other[:, :, JW * jq : JW * (jq + 1)].rearrange("p t (g i) -> p g t i", i=2),
                in1=cof[b, jq][:].rearrange("p t (g i) -> p g t i", i=2),
                op=op,
            )

        def quantize_h(name, b, j0, j1):
            if j0 == 0:
                codes[name, b] = kept([P, S], U32, "%s_codes%d" % (name, b))
                scales[name, b] = kept([P, S], U8, "%s_scales%d" % (name, b))
            nc.vector.quantize_mx(
                out=codes[name, b][:, j0:j1].bitcast(FP8X4),
                scales=scales[name, b][:, j0:j1],
                in_=h_rounded[name, b][:, PACK * j0 : PACK * j1],
            )

        ys = {}

        def y_passes(jq, operands):
            js = slice(JW * jq, JW * (jq + 1))
            opens = jq not in ys
            if opens:
                ys[jq] = psum.tile([P, N // P, JW], F32, name="y", tag="bank%d" % (4 + jq))
            y = ys[jq]
            passes = [(b, name, c) for b, name in operands for c in range(N // P)]
            for n, (b, name, c) in enumerate(passes):
                cols = slice(P * c, P * (c + 1))
                if name == "h1":
                    lhsT = w4[:, b, 2 * P * c : 2 * P * (c + 1)].bitcast(FP4X4)
                    lhsT_scale = w4_sc[:, b, cols]
                else:
                    lhsT = codes["w5", b, 0][:, cols].bitcast(FP8X4)
                    lhsT_scale = scales["w5", b, 0][:, cols]
                nc.tensor.matmul_mx(
                    out=y[:, c, :],
                    lhsT=lhsT,
                    lhsT_scale=lhsT_scale,
                    rhs=codes[name, b][:, js].bitcast(FP8X4),
                    rhs_scale=scales[name, b][:, js],
                    start=(opens and n == 0),
                    stop=(not opens and n == len(passes) - 1),
                )

        def second_stage(jq):
            js = slice(JW * jq, JW * (jq + 1))
            y_passes(jq, [(1, "h2")])
            y = ys[jq]
            scores = work.tile([P, N // P, JW], F32, name="scores", bufs=JQ)
            for c in range(N // P):
                nc.scalar.activation(out=scores[:, c, :], in_=y[:, c, :], func=ACT.Tanh, bias=b5_sb[:, c : c + 1])
            nc.sync.dma_start(out=out[:, js].rearrange("(c p) j -> p c j", p=P), in_=scores[:])

        nc.sync.dma_start(lists[0][:], offs)
        nc.sync.dma_start(lists[2][:], offs3)
        nc.sync.dma_start(lists[1][:], offs2)
        nc.sync.dma_start(out=b1_sb[:], in_=b1.rearrange("(b p t) -> p b t", b=2, t=PACK))
        load_tab(0)
        load_w("w1", w1, 0, 0)
        for q in range(QUADS):
            nc.sync.dma_start(
                out=tab_sc[32 * q : 32 * q + 8, :].bitcast(I32), in_=tab_scales[:, 4 * q : 4 * q + 4, :].bitcast(I32)
            )
        load_w("w1", w1, 1, 0)
        load_tab(1)
        load_w("w3", w3, 0, 0)
        nc.sync.dma_start(out=b3_sb[:], in_=b3.rearrange("(b p t) -> p b t", b=2, t=PACK))
        load_w("w3", w3, 1, 0)
        for q in range(QUADS):
            nc.sync.dma_start(
                out=w2_sc_raw[32 * q : 32 * q + 8, :].bitcast(I32), in_=w2_scales[:, 4 * q : 4 * q + 4, :].bitcast(I32)
            )
        nc.sync.dma_start(out=w2_raw[:].bitcast(I32), in_=w2_words.rearrange("a p c i -> p a (c i)").bitcast(I32))
        load_w("w1", w1, 0, 1)
        load_w("w1", w1, 1, 1)
        load_w("w3", w3, 0, 1)
        load_w("w3", w3, 1, 1)
        load_w("w5", w5, 0, 0)
        load_w("w5", w5, 1, 0)
        for q in range(QUADS):
            nc.sync.dma_start(
                out=w4_sc[32 * q : 32 * q + 4, :, :].bitcast(I32),
                in_=w4_scales[:, 4 * q : 4 * q + 4, :].rearrange("a r n -> r a n").bitcast(I32),
            )
        nc.sync.dma_start(out=w4[:].bitcast(I32), in_=w4_words.rearrange("a p x -> p a x").bitcast(I32))
        with nc.allow_non_contiguous_dma(reason="one bias value for each partition and output tile"):
            nc.sync.dma_start(out=b5_sb[:], in_=b5.rearrange("(c p) -> p c", p=P))
        gather_words(0, 0)
        gather_words(2, 0)
        gather_words(1, 0)
        gather_scales(0)
        gather_scales(2)
        gather_scales(1)
        round_w("w1", 0, 0, "SS")
        quantize_w("w1", 0, 0)
        round_w("w1", 1, 0, "SS")
        quantize_w("w1", 1, 0)
        gather_words(0, 1)
        gather_words(2, 1)
        gather_words(1, 1)
        round_w("w3", 0, 0, "SS")
        drug_stage(0)
        quantize_w("w3", 0, 0)
        round_w("w3", 1, 0, "VV")
        quantize_w("w3", 1, 0)
        sol_stage(0)
        deal_w2()
        for jq in range(JQ):
            cof_stage(0, jq)
        round_w("w1", 0, 1, "SS")
        quantize_w("w1", 0, 1)
        round_w("w1", 1, 1, "SV")
        quantize_w("w1", 1, 1)
        round_w("w3", 0, 1, "SS")
        drug_stage(1)
        quantize_w("w3", 0, 1)
        round_w("w3", 1, 1, "VV")
        quantize_w("w3", 1, 1)
        sol_stage(1)
        for jq in range(JQ):
            combine("h1", 0, jq)
        for jq in range(JQ):
            combine("h2", 0, jq)
        quantize_h("h1", 0, 0, S)
        quantize_h("h2", 0, 0, S)
        for jq in range(JQ):
            cof_stage(1, jq)
        round_w("w5", 0, 0, "VV")
        quantize_w("w5", 0, 0)
        round_w("w5", 1, 0, "SS")
        quantize_w("w5", 1, 0)
        for jq in range(JQ):
            combine("h1", 1, jq)
        quantize_h("h1", 1, 0, S)
        for jq in range(JQ):
            y_passes(jq, [(0, "h1"), (0, "h2"), (1, "h1")])
        for jq in range(JQ):
            combine("h2", 1, jq)
            if jq > 0:
                quantize_h("h2", 1, JW * (jq - 1), JW * jq)
                second_stage(jq - 1)
        quantize_h("h2", 1, JW * (JQ - 1), S)
        second_stage(JQ - 1)
